import numpy as np
import ml_dtypes


def mxq(x, axis, fmt="e4m3"):
    dtype, down = {"e4m3": (ml_dtypes.float8_e4m3fn, 7), "e5m2": (ml_dtypes.float8_e5m2, 14)}[fmt]
    v = np.moveaxis(np.asarray(x, np.float32).astype(ml_dtypes.bfloat16).astype(np.float64), axis, -1)
    blocks = v.reshape(v.shape[:-1] + (-1, 32))
    amax = np.abs(blocks).max(-1, keepdims=True)
    byte = np.maximum(np.where(amax > 0, np.frexp(amax)[1] - 1 + 127, 0) - down, 1)
    scale = np.exp2(byte - 127.0)
    codes = (blocks / scale).astype(np.float32).astype(dtype).astype(np.float64)
    return np.moveaxis((codes * scale).reshape(v.shape), -1, axis)


WIDE = False


def mx_kscale(k):
    if not WIDE:
        return np.ones(k)
    levels = np.array([10, -10, 5, -5, 0])
    if k % 512:
        return np.exp2(np.random.permutation(np.resize(levels, k // 32))).repeat(32)
    a = np.empty((k // 512, 16))
    for p in range(k // 512):
        a[p, :8] = np.random.permutation(np.resize(levels, 8))
        for g in range(8):
            far = levels[np.abs(levels - a[p, g]) >= 10]
            a[p, g + 8] = far[np.random.randint(len(far))]
    return np.exp2(a.ravel()).repeat(32)


def f64(x):
    return np.asarray(x).astype(np.float64)


def striped(idx):
    return np.tile(idx.reshape(-1, 16).T, (8, 1)).astype(np.uint16)


def unstriped(offs):
    return offs[:16].T.reshape(-1).astype(np.int64)


E2M1 = np.array([0.0, 0.5, 1.0, 1.5, 2.0, 3.0, 4.0, 6.0, -0.0, -0.5, -1.0, -1.5, -2.0, -3.0, -4.0, -6.0])


def pack_weight(w, fmt):
    k, n = w.shape
    w = f64(np.asarray(w, np.float32).astype(ml_dtypes.bfloat16)).reshape(k // 32, 32, n)
    amax = np.abs(w).max(1)
    if fmt == "e4m3":
        byte = np.frexp(amax)[1] - 1 + 127 - 7
    else:
        mant, ex = np.frexp(amax / 6.0)
        byte = np.where(mant > 0.5, ex, ex - 1) + 127
    byte = np.clip(np.where(amax > 0, byte, 1), 1, 254)
    scaled = (w * np.exp2(127.0 - byte)[:, None, :]).reshape(k, n).astype(np.float32)
    by_word = np.ascontiguousarray(scaled.reshape(k // 512, 128, 4, n).transpose(0, 1, 3, 2))
    if fmt == "e4m3":
        words = by_word.astype(ml_dtypes.float8_e4m3fn).view(np.uint8)
    else:
        c = by_word.astype(ml_dtypes.float4_e2m1fn).view(np.uint8) & 0xF
        words = (c[..., 0::2] | (c[..., 1::2] << 4)).reshape(k // 512, 128, 2 * n)
    return np.ascontiguousarray(words), np.ascontiguousarray(byte.astype(np.uint8).reshape(k // 512, 16, n))


def unpack_weight(words, scales, fmt):
    g, _, n = scales.shape
    words = np.ascontiguousarray(words).reshape(g, 128, n, -1)
    if fmt == "e4m3":
        vals = words.view(ml_dtypes.float8_e4m3fn).astype(np.float64)
    else:
        nib = np.empty((g, 128, n, 4), np.uint8)
        nib[..., 0::2] = words & 0xF
        nib[..., 1::2] = words >> 4
        vals = E2M1[nib]
    vals = vals * np.repeat(np.exp2(scales.astype(np.float64) - 127.0), 8, axis=1)[..., None]
    return vals.transpose(0, 1, 3, 2).reshape(g * 512, n)


def gelu(v):
    return 0.5 * v * (1.0 + np.tanh(np.sqrt(2.0 / np.pi) * (v + 0.044715 * v**3)))


K, T, S, H, T3, S2, P = 1024, 4096, 1024, 512, 2048, 1024, 512

def setup_inputs():
    n = np.random.standard_normal
    s = mx_kscale(K)[:, None]
    u = mx_kscale(H)[:, None]
    tab_words, tab_scales = pack_weight(n((K, T)) * s, "e4m3")
    tab2_words, tab2_scales = pack_weight(n((H, T3)) / np.sqrt(H) / u, "e4m3")
    return {
        "tab_words": tab_words, "tab_scales": tab_scales,
        "tab2_words": tab2_words, "tab2_scales": tab2_scales,
        "offs": striped(np.random.permutation(T)[:S]),
        "offs2": striped(np.random.permutation(T3)[:S2]),
        "pos1": striped(np.random.permutation(S)[:P]),
        "pos2": striped(np.random.permutation(S)[:P]),
        "w1": (0.55 * n((K, H)) / np.sqrt(K) / s).astype(np.float32),
        "gain": (np.exp(0.3 * n(H)) * u[:, 0]).astype(np.float32),
        "plans": (0.5 * n((H, P)) * u).astype(np.float32),
        "mood": np.exp(0.3 * n(H)).astype(np.float32),
        "quiet": (0.5 * n((S2, P))).astype(np.float32),
        "care": np.exp(0.3 * n(S2)).astype(np.float32),
    }

def reference(tab_words, tab_scales, tab2_words, tab2_scales, offs, offs2, pos1, pos2,
              w1, gain, plans, mood, quiet, care):
    v = unpack_weight(tab_words, tab_scales, "e4m3")[:, unstriped(offs)]
    v2 = unpack_weight(tab2_words, tab2_scales, "e4m3")[:, unstriped(offs2)]
    w1q = mxq(f64(w1), 0, "e4m3")
    h = np.cos(w1q.T @ v) * f64(gain)[:, None]
    x1 = mxq(h[:, unstriped(pos1)], 0, "e4m3")
    x2 = mxq((h[:, unstriped(pos2)] + f64(plans)) * f64(mood)[:, None], 0, "e4m3")
    e1 = v2.T @ x1
    e2 = v2.T @ x2
    return (e1 + f64(quiet)) * f64(care)[:, None] + e2

@@ -1,0 +1,190 @@
+import math
+from contextlib import ExitStack
+
+import concourse.mybir as mybir
+from concourse.masks import make_identity
+
+K, T, S, H, T3, S2, PAIRS = 1024, 4096, 1024, 512, 2048, 1024, 512
+FLOPS = 2 * K * H * S + 2 * 2 * H * S2 * PAIRS
+
+F32 = mybir.dt.float32
+BF16 = mybir.dt.bfloat16
+I32 = mybir.dt.int32
+U32 = mybir.dt.uint32
+U16 = mybir.dt.uint16
+U8 = mybir.dt.uint8
+FP8X4 = mybir.dt.float8_e4m3fn_x4
+ALU = mybir.AluOpType
+ACT = mybir.ActivationFunctionType
+
+P = 128
+PACK = 4
+BANK = 512
+PASSES = K // (P * PACK)
+M_TILES = S2 // P
+QUADS = 4
+V2_ROW = 8
+M_SPLIT = 80
+
+
+def tile_list_dorm_bed_scores_kernel(tc, tab_words, tab_scales, tab2_words, tab2_scales, offs, offs2,
+                                               pos1, pos2, w1, gain, plans, mood, quiet, care, out):
+    nc = tc.nc
+    with ExitStack() as ctx:
+        lists = ctx.enter_context(tc.tile_pool(name="lists", bufs=1))
+        keep = ctx.enter_context(tc.tile_pool(name="keep", bufs=1))
+        ring = ctx.enter_context(tc.tile_pool(name="ring", bufs=2))
+        psum = ctx.enter_context(tc.psum_pool(name="psum", bufs=1))
+
+        idx = lists.tile([P, S // 16], U16, name="idx")
+        idx2 = lists.tile([P, S2 // 16], U16, name="idx2")
+        p1 = lists.tile([P, PAIRS // 16], U16, name="p1")
+        p2 = lists.tile([P, PAIRS // 16], U16, name="p2")
+
+        v_words = [keep.tile([P, T], U32, name="v_words%d" % a) for a in range(PASSES)]
+        v_scales = keep.tile([P, T], U8, name="v_scales")
+        v2_words = keep.tile([P, T3], U32, name="v2_words")
+        v2_scales = keep.tile([P, T3], U8, name="v2_scales")
+        w_raw = [keep.tile([P, PACK, H], F32, name="w_raw%d" % a) for a in range(PASSES)]
+        gain_sb = keep.tile([P, PACK], F32, name="gain_sb")
+        mood_sb = keep.tile([P, PACK], F32, name="mood_sb")
+        plans_sb = keep.tile([P, PACK, PAIRS], F32, name="plans_sb")
+        quiet_sb = keep.tile([P, M_TILES, PAIRS], F32, name="quiet_sb")
+        care_rows = keep.tile([P, P], F32, name="care_rows")
+        ident = keep.tile([P, P], F32, name="ident")
+
+        nc.vector.memset(v_scales[:].bitcast(I32), 0)
+        nc.vector.memset(v2_scales[:].bitcast(I32), 0)
+        nc.vector.memset(care_rows[:], 0.0)
+        make_identity(nc, ident[:])
+
+        nc.sync.dma_start(idx[:], offs)
+        nc.sync.dma_start(idx2[:], offs2)
+        for q in range(QUADS):
+            nc.scalar.dma_start(out=v_scales[32 * q: 32 * q + 4 * PASSES, :].bitcast(I32),
+                                in_=tab_scales[:, 4 * q: 4 * q + 4, :].bitcast(I32))
+        for a in range(PASSES):
+            nc.sync.dma_start(out=v_words[a][:].bitcast(I32),
+                              in_=tab_words[a].rearrange("p n i -> p (n i)").bitcast(I32))
+            nc.sync.dma_start(out=w_raw[a][:],
+                              in_=w1[a * P * PACK: (a + 1) * P * PACK, :].rearrange("(p j) c -> p j c", j=PACK))
+        for q in range(QUADS):
+            nc.scalar.dma_start(out=v2_scales[32 * q + V2_ROW: 32 * q + V2_ROW + 4, :].bitcast(I32),
+                                in_=tab2_scales[0, 4 * q: 4 * q + 4, :].bitcast(I32))
+        nc.scalar.dma_start(out=care_rows[0:M_TILES, :], in_=care.rearrange("(b p) -> b p", p=P))
+        nc.sync.dma_start(out=v2_words[:].bitcast(I32),
+                          in_=tab2_words[0].rearrange("p n i -> p (n i)").bitcast(I32))
+        nc.sync.dma_start(p2[:], pos2)
+        nc.sync.dma_start(p1[:], pos1)
+        nc.sync.dma_start(out=gain_sb[:], in_=gain.rearrange("(p t) -> p t", t=PACK))
+        nc.sync.dma_start(out=mood_sb[:], in_=mood.rearrange("(p t) -> p t", t=PACK))
+        nc.sync.dma_start(out=plans_sb[:], in_=plans.rearrange("(p t) j -> p t j", t=PACK))
+        nc.sync.dma_start(out=quiet_sb[:], in_=quiet.rearrange("(b p) j -> p b j", p=P))
+
+        def bank(b):
+            return psum.tile([P, BANK], F32, name="bank%d" % b)
+
+        vg_scales = keep.tile([P, S], U8, name="vg_scales", align_bytes=64)
+        v2g_scales = keep.tile([P, S2], U8, name="v2g_scales", align_bytes=64)
+        vg_words = [keep.tile([P, S], U32, name="vg_words%d" % a, align_bytes=64) for a in range(PASSES)]
+        v2g_words = keep.tile([P, S2], U32, name="v2g_words", align_bytes=64)
+        w_bf = [keep.tile([P, PACK * H], BF16, name="w_bf%d" % a, align_bytes=64) for a in range(PASSES)]
+        w_codes = [keep.tile([P, H], U32, name="w_codes%d" % a, align_bytes=64) for a in range(PASSES)]
+        w_scales = [keep.tile([P, H], U8, name="w_scales%d" % a, align_bytes=64) for a in range(PASSES)]
+
+        nc.vector.tensor_copy(vg_scales[:], v_scales[:].indirect(idx[:]))
+        z = [[bank(2 * t + s) for s in range(2)] for t in range(PACK)]
+        for a in range(PASSES):
+            nc.vector.tensor_copy(vg_words[a][:], v_words[a][:].indirect(idx[:]))
+            if a == 0:
+                nc.vector.tensor_copy(v2g_scales[:], v2_scales[:].indirect(idx2[:]))
+            dst = w_bf[a][:].rearrange("p (t m j) -> p m j t", t=PACK, j=PACK)
+            src = w_raw[a][:].rearrange("p j (m t) -> p m j t", t=PACK)
+            if a == 0:
+                nc.scalar.copy(out=dst, in_=src)
+                nc.vector.quantize_mx(out=w_codes[a][:].bitcast(FP8X4), scales=w_scales[a][:], in_=w_bf[a][:])
+            else:
+                nc.vector.tensor_copy(out=dst[:, :M_SPLIT], in_=src[:, :M_SPLIT])
+                nc.scalar.copy(out=dst[:, M_SPLIT:], in_=src[:, M_SPLIT:])
+            for t in range(PACK):
+                cols = slice(t * P, (t + 1) * P)
+                if a == 1:
+                    nc.vector.quantize_mx(out=w_codes[a][:, cols].bitcast(FP8X4), scales=w_scales[a][:, cols],
+                                          in_=w_bf[a][:, t * BANK: (t + 1) * BANK])
+                for s in range(2):
+                    n = slice(s * BANK, (s + 1) * BANK)
+                    nc.tensor.matmul_mx(out=z[t][s][:], lhsT=w_codes[a][:, cols].bitcast(FP8X4),
+                                        lhsT_scale=w_scales[a][:, cols],
+                                        rhs=vg_words[a][:, n].bitcast(FP8X4), rhs_scale=vg_scales[4 * a:, n],
+                                        start=(a == 0), stop=(a == PASSES - 1))
+
+        nc.vector.tensor_copy(v2g_words[:], v2_words[:].indirect(idx2[:]))
+
+        cosz = [keep.tile([P, S], F32, name="cosz%d" % t) for t in range(PACK)]
+        for t in range(PACK):
+            turns = ring.tile([P, S], F32, name="turns", bufs=3)
+            for s in range(2):
+                nc.scalar.activation(out=turns[:, s * BANK: (s + 1) * BANK], in_=z[t][s][:], func=ACT.Copy,
+                                     bias=0.25, scale=1.0 / (2.0 * math.pi))
+            whole = ring.tile([P, S], I32, name="whole")
+            nc.vector.tensor_copy(out=whole[:], in_=turns[:])
+            frac = ring.tile([P, S], F32, name="frac")
+            nc.vector.tensor_tensor(out=frac[:], in0=turns[:], in1=whole[:], op=ALU.subtract)
+            nc.scalar.activation(out=cosz[t][:], in_=frac[:], func=ACT.Sin, scale=2.0 * math.pi)
+
+        care_ps = bank(0)
+        nc.tensor.transpose(care_ps[:, 0:P], care_rows[:], ident[:])
+        care_sb = keep.tile([P, M_TILES], F32, name="care_sb")
+        nc.scalar.copy(out=care_sb[:], in_=care_ps[:, 0:M_TILES])
+
+        gm = keep.tile([P, PACK], F32, name="gm")
+        nc.vector.tensor_tensor(out=gm[:], in0=gain_sb[:], in1=mood_sb[:], op=ALU.mult)
+        for t in range(PACK):
+            nc.scalar.activation(out=plans_sb[:, t, :], in_=plans_sb[:, t, :], func=ACT.Copy,
+                                 scale=mood_sb[:, t: t + 1])
+
+        def interleave_quantise(planes, tag):
+            woven = keep.tile([P, PACK * PAIRS], BF16, name="woven" + tag, align_bytes=64)
+            nc.scalar.copy(out=woven[:].rearrange("p (c i t) -> p c t i", i=4, t=PACK),
+                           in_=planes[:].rearrange("p t (c i) -> p c t i", i=4))
+            codes = keep.tile([P, PAIRS], U32, name="codes" + tag, align_bytes=64)
+            scales = keep.tile([P, PAIRS], U8, name="scales" + tag, align_bytes=64)
+            return woven, codes, scales
+
+        planes2 = keep.tile([P, PACK, PAIRS], BF16, name="planes2")
+        for t in range(PACK):
+            g2 = keep.tile([P, PAIRS], F32, name="g2_%d" % t)
+            nc.vector.tensor_copy(g2[:], cosz[t][:].indirect(p2[:]))
+            nc.vector.scalar_tensor_tensor(out=planes2[:, t, :], in0=g2[:], scalar=gm[:, t: t + 1],
+                                           in1=plans_sb[:, t, :], op0=ALU.mult, op1=ALU.add)
+        woven2, codes2, scales2 = interleave_quantise(planes2, "2")
+
+        planes1 = keep.tile([P, PACK, PAIRS], BF16, name="planes1")
+        for t in range(PACK):
+            g1 = keep.tile([P, PAIRS], F32, name="g1_%d" % t)
+            nc.vector.tensor_copy(g1[:], cosz[t][:].indirect(p1[:]))
+            nc.scalar.activation(out=planes1[:, t, :], in_=g1[:], func=ACT.Copy, scale=gain_sb[:, t: t + 1])
+            if t == 2:
+                nc.vector.quantize_mx(out=codes2[:].bitcast(FP8X4), scales=scales2[:], in_=woven2[:])
+        woven1, codes1, scales1 = interleave_quantise(planes1, "1")
+
+        def score(b, codes, scales):
+            e = bank(b)
+            cols = slice(b * P, (b + 1) * P)
+            nc.tensor.matmul_mx(out=e[:], lhsT=v2g_words[:, cols].bitcast(FP8X4),
+                                lhsT_scale=v2g_scales[V2_ROW:, cols],
+                                rhs=codes[:].bitcast(FP8X4), rhs_scale=scales[:], start=True, stop=True)
+            return e
+
+        for b in range(M_TILES):
+            e2 = score(b, codes2, scales2)
+            nc.vector.scalar_tensor_tensor(out=quiet_sb[:, b, :], in0=quiet_sb[:, b, :], scalar=care_sb[:, b: b + 1],
+                                           in1=e2[:], op0=ALU.mult, op1=ALU.add)
+            if b == 5:
+                nc.vector.quantize_mx(out=codes1[:].bitcast(FP8X4), scales=scales1[:], in_=woven1[:])
+        for b in range(M_TILES):
+            e1 = score(b, codes1, scales1)
+            res = ring.tile([P, PAIRS], F32, name="res", bufs=M_TILES)
+            nc.vector.scalar_tensor_tensor(out=res[:], in0=e1[:], scalar=care_sb[:, b: b + 1],
+                                           in1=quiet_sb[:, b, :], op0=ALU.mult, op1=ALU.add)
+            nc.sync.dma_start(out=out[b * P: (b + 1) * P, :], in_=res[:])

@@ -24,7 +24,8 @@ PASSES = K // (P * PACK)
 M_TILES = S2 // P
 QUADS = 4
 V2_ROW = 8
-M_SPLIT = 80
+M_SPLIT = 40
+POOL_TILES = 0
 
 
 def tile_list_dorm_bed_scores_kernel(tc, tab_words, tab_scales, tab2_words, tab2_scales, offs, offs2,
@@ -45,7 +46,8 @@ def tile_list_dorm_bed_scores_kernel(tc, tab_words, tab_scales, tab2_words, tab2
         v_scales = keep.tile([P, T], U8, name="v_scales")
         v2_words = keep.tile([P, T3], U32, name="v2_words")
         v2_scales = keep.tile([P, T3], U8, name="v2_scales")
-        w_raw = [keep.tile([P, PACK, H], F32, name="w_raw%d" % a) for a in range(PASSES)]
+        w_first = keep.tile([P, PACK, H], F32, name="w_first")
+        w_last = [keep.tile([P, PACK, H // 2], F32, name="w_last%d" % u) for u in range(2)]
         gain_sb = keep.tile([P, PACK], F32, name="gain_sb")
         mood_sb = keep.tile([P, PACK], F32, name="mood_sb")
         plans_sb = keep.tile([P, PACK, PAIRS], F32, name="plans_sb")
@@ -58,26 +60,35 @@ def tile_list_dorm_bed_scores_kernel(tc, tab_words, tab_scales, tab2_words, tab2
         nc.vector.memset(care_rows[:], 0.0)
         make_identity(nc, ident[:])
 
+        def load_words(a, cols):
+            nc.sync.dma_start(out=v_words[a][:, cols].bitcast(I32),
+                              in_=tab_words[a].rearrange("p n i -> p (n i)").bitcast(I32)[:, cols])
+
+        def load_w1(dst, a, cols):
+            nc.sync.dma_start(out=dst[:],
+                              in_=w1[a * P * PACK: (a + 1) * P * PACK, cols].rearrange("(p j) c -> p j c", j=PACK))
+
         nc.sync.dma_start(idx[:], offs)
+        load_words(0, slice(0, T // 2))
+        for q in range(QUADS):
+            nc.sync.dma_start(out=v_scales[32 * q: 32 * q + 4 * PASSES, :].bitcast(I32),
+                              in_=tab_scales[:, 4 * q: 4 * q + 4, :].bitcast(I32))
+        load_words(0, slice(T // 2, T))
         nc.sync.dma_start(idx2[:], offs2)
+        load_w1(w_first, 0, slice(0, H))
         for q in range(QUADS):
-            nc.scalar.dma_start(out=v_scales[32 * q: 32 * q + 4 * PASSES, :].bitcast(I32),
-                                in_=tab_scales[:, 4 * q: 4 * q + 4, :].bitcast(I32))
-        for a in range(PASSES):
-            nc.sync.dma_start(out=v_words[a][:].bitcast(I32),
-                              in_=tab_words[a].rearrange("p n i -> p (n i)").bitcast(I32))
-            nc.sync.dma_start(out=w_raw[a][:],
-                              in_=w1[a * P * PACK: (a + 1) * P * PACK, :].rearrange("(p j) c -> p j c", j=PACK))
-        for q in range(QUADS):
-            nc.scalar.dma_start(out=v2_scales[32 * q + V2_ROW: 32 * q + V2_ROW + 4, :].bitcast(I32),
-                                in_=tab2_scales[0, 4 * q: 4 * q + 4, :].bitcast(I32))
-        nc.scalar.dma_start(out=care_rows[0:M_TILES, :], in_=care.rearrange("(b p) -> b p", p=P))
+            nc.sync.dma_start(out=v2_scales[32 * q + V2_ROW: 32 * q + V2_ROW + 4, :].bitcast(I32),
+                              in_=tab2_scales[0, 4 * q: 4 * q + 4, :].bitcast(I32))
+        load_words(1, slice(0, T))
+        for u in range(2):
+            load_w1(w_last[u], 1, slice(u * H // 2, (u + 1) * H // 2))
         nc.sync.dma_start(out=v2_words[:].bitcast(I32),
                           in_=tab2_words[0].rearrange("p n i -> p (n i)").bitcast(I32))
-        nc.sync.dma_start(p2[:], pos2)
         nc.sync.dma_start(p1[:], pos1)
+        nc.sync.dma_start(p2[:], pos2)
         nc.sync.dma_start(out=gain_sb[:], in_=gain.rearrange("(p t) -> p t", t=PACK))
         nc.sync.dma_start(out=mood_sb[:], in_=mood.rearrange("(p t) -> p t", t=PACK))
+        nc.sync.dma_start(out=care_rows[0:M_TILES, :], in_=care.rearrange("(b p) -> b p", p=P))
         nc.sync.dma_start(out=plans_sb[:], in_=plans.rearrange("(p t) j -> p t j", t=PACK))
         nc.sync.dma_start(out=quiet_sb[:], in_=quiet.rearrange("(b p) j -> p b j", p=P))
 
@@ -99,13 +110,15 @@ def tile_list_dorm_bed_scores_kernel(tc, tab_words, tab_scales, tab2_words, tab2
             if a == 0:
                 nc.vector.tensor_copy(v2g_scales[:], v2_scales[:].indirect(idx2[:]))
             dst = w_bf[a][:].rearrange("p (t m j) -> p m j t", t=PACK, j=PACK)
-            src = w_raw[a][:].rearrange("p j (m t) -> p m j t", t=PACK)
             if a == 0:
-                nc.scalar.copy(out=dst, in_=src)
+                nc.scalar.copy(out=dst, in_=w_first[:].rearrange("p j (m t) -> p m j t", t=PACK))
                 nc.vector.quantize_mx(out=w_codes[a][:].bitcast(FP8X4), scales=w_scales[a][:], in_=w_bf[a][:])
             else:
-                nc.vector.tensor_copy(out=dst[:, :M_SPLIT], in_=src[:, :M_SPLIT])
-                nc.scalar.copy(out=dst[:, M_SPLIT:], in_=src[:, M_SPLIT:])
+                src = [w[:].rearrange("p j (m t) -> p m j t", t=PACK) for w in w_last]
+                half = P // 2
+                nc.scalar.copy(out=dst[:, :half], in_=src[0])
+                nc.vector.tensor_copy(out=dst[:, half: half + M_SPLIT], in_=src[1][:, :M_SPLIT])
+                nc.scalar.copy(out=dst[:, half + M_SPLIT:], in_=src[1][:, M_SPLIT:])
             for t in range(PACK):
                 cols = slice(t * P, (t + 1) * P)
                 if a == 1:
@@ -118,55 +131,70 @@ def tile_list_dorm_bed_scores_kernel(tc, tab_words, tab_scales, tab2_words, tab2
                                         rhs=vg_words[a][:, n].bitcast(FP8X4), rhs_scale=vg_scales[4 * a:, n],
                                         start=(a == 0), stop=(a == PASSES - 1))
 
-        nc.vector.tensor_copy(v2g_words[:], v2_words[:].indirect(idx2[:]))
 
+        per_turn = 1.0 / (2.0 * math.pi)
         cosz = [keep.tile([P, S], F32, name="cosz%d" % t) for t in range(PACK)]
-        for t in range(PACK):
-            turns = ring.tile([P, S], F32, name="turns", bufs=3)
+        whole0 = [keep.tile([P, BANK], I32, name="whole0_%d" % s) for s in range(2)]
+        for s in range(2):
+            nc.vector.tensor_scalar(out=whole0[s][:], in0=z[0][s][:], scalar1=per_turn, scalar2=0.25,
+                                    op0=ALU.mult, op1=ALU.add)
+        for s in range(2):
+            frac0 = ring.tile([P, BANK], F32, name="turns")
+            nc.vector.scalar_tensor_tensor(out=frac0[:], in0=z[0][s][:], scalar=per_turn, in1=whole0[s][:],
+                                           op0=ALU.mult, op1=ALU.subtract)
+            nc.scalar.activation(out=cosz[0][:, s * BANK: (s + 1) * BANK], in_=frac0[:], func=ACT.Sin,
+                                 scale=2.0 * math.pi, bias=0.5 * math.pi)
+        nc.vector.tensor_copy(v2g_words[:], v2_words[:].indirect(idx2[:]))
+        fracs = {}
+        for t in range(1, PACK):
+            turns = ring.tile([P, S], F32, name="turns")
             for s in range(2):
-                nc.scalar.activation(out=turns[:, s * BANK: (s + 1) * BANK], in_=z[t][s][:], func=ACT.Copy,
-                                     bias=0.25, scale=1.0 / (2.0 * math.pi))
-            whole = ring.tile([P, S], I32, name="whole")
-            nc.vector.tensor_copy(out=whole[:], in_=turns[:])
-            frac = ring.tile([P, S], F32, name="frac")
-            nc.vector.tensor_tensor(out=frac[:], in0=turns[:], in1=whole[:], op=ALU.subtract)
-            nc.scalar.activation(out=cosz[t][:], in_=frac[:], func=ACT.Sin, scale=2.0 * math.pi)
+                nc.scalar.activation(out=turns[:, s * BANK: (s + 1) * BANK], in_=z[t][s][:], func=ACT.Abs,
+                                     scale=per_turn)
+            whole = keep.tile([P, S], U32, name="whole%d" % t)
+            nc.scalar.activation(out=whole[:], in_=turns[:], func=ACT.Copy, bias=0.25)
+            fracs[t] = keep.tile([P, S], F32, name="frac%d" % t)
+            nc.vector.scalar_tensor_tensor(out=fracs[t][:], in0=turns[:], scalar=0.25, in1=whole[:].bitcast(I32),
+                                           op0=ALU.add, op1=ALU.subtract)
+        for t in range(1, PACK):
+            nc.scalar.activation(out=cosz[t][:], in_=fracs[t][:], func=ACT.Sin, scale=2.0 * math.pi)
 
         care_ps = bank(0)
         nc.tensor.transpose(care_ps[:, 0:P], care_rows[:], ident[:])
         care_sb = keep.tile([P, M_TILES], F32, name="care_sb")
         nc.scalar.copy(out=care_sb[:], in_=care_ps[:, 0:M_TILES])
 
-        gm = keep.tile([P, PACK], F32, name="gm")
-        nc.vector.tensor_tensor(out=gm[:], in0=gain_sb[:], in1=mood_sb[:], op=ALU.mult)
-        for t in range(PACK):
-            nc.scalar.activation(out=plans_sb[:, t, :], in_=plans_sb[:, t, :], func=ACT.Copy,
-                                 scale=mood_sb[:, t: t + 1])
+        def round_into(pairs, t, values, factor):
+            nc.scalar.activation(out=pairs[:, t // 2, :, t % 2], in_=values, func=ACT.Copy,
+                                 scale=factor[:, t: t + 1])
 
-        def interleave_quantise(planes, tag):
+        def weave(pairs, tag):
             woven = keep.tile([P, PACK * PAIRS], BF16, name="woven" + tag, align_bytes=64)
-            nc.scalar.copy(out=woven[:].rearrange("p (c i t) -> p c t i", i=4, t=PACK),
-                           in_=planes[:].rearrange("p t (c i) -> p c t i", i=4))
+            nc.scalar.copy(out=woven[:].bitcast(U32).rearrange("p (j h) -> p j h", h=2),
+                           in_=pairs[:].rearrange("p h j e -> p h (j e)").bitcast(U32).rearrange("p h j -> p j h"))
             codes = keep.tile([P, PAIRS], U32, name="codes" + tag, align_bytes=64)
             scales = keep.tile([P, PAIRS], U8, name="scales" + tag, align_bytes=64)
             return woven, codes, scales
 
-        planes2 = keep.tile([P, PACK, PAIRS], BF16, name="planes2")
+        pairs1 = keep.tile([P, 2, PAIRS, 2], BF16, name="pairs1")
         for t in range(PACK):
-            g2 = keep.tile([P, PAIRS], F32, name="g2_%d" % t)
-            nc.vector.tensor_copy(g2[:], cosz[t][:].indirect(p2[:]))
-            nc.vector.scalar_tensor_tensor(out=planes2[:, t, :], in0=g2[:], scalar=gm[:, t: t + 1],
-                                           in1=plans_sb[:, t, :], op0=ALU.mult, op1=ALU.add)
-        woven2, codes2, scales2 = interleave_quantise(planes2, "2")
-
-        planes1 = keep.tile([P, PACK, PAIRS], BF16, name="planes1")
-        for t in range(PACK):
-            g1 = keep.tile([P, PAIRS], F32, name="g1_%d" % t)
+            g1 = keep.tile([P, PAIRS], F32, name="whole1" if t == 0 else "g1_%d" % t)
             nc.vector.tensor_copy(g1[:], cosz[t][:].indirect(p1[:]))
-            nc.scalar.activation(out=planes1[:, t, :], in_=g1[:], func=ACT.Copy, scale=gain_sb[:, t: t + 1])
-            if t == 2:
-                nc.vector.quantize_mx(out=codes2[:].bitcast(FP8X4), scales=scales2[:], in_=woven2[:])
-        woven1, codes1, scales1 = interleave_quantise(planes1, "1")
+            round_into(pairs1, t, g1[:], gain_sb)
+        woven1, codes1, scales1 = weave(pairs1, "1")
+
+        pairs2 = keep.tile([P, 2, PAIRS, 2], BF16, name="pairs2")
+        for t in range(PACK):
+            if t == 3:
+                nc.vector.quantize_mx(out=codes1[:].bitcast(FP8X4), scales=scales1[:], in_=woven1[:])
+                g2 = keep.tile([P, PAIRS], F32, name="woven1", align_bytes=64)
+            else:
+                g2 = keep.tile([P, PAIRS], F32, name="frac3" if t == 2 else "g2_%d" % t)
+            nc.vector.tensor_copy(g2[:], cosz[t][:].indirect(p2[:]))
+            nc.vector.scalar_tensor_tensor(out=plans_sb[:, t, :], in0=g2[:], scalar=gain_sb[:, t: t + 1],
+                                           in1=plans_sb[:, t, :], op0=ALU.mult, op1=ALU.add)
+            round_into(pairs2, t, plans_sb[:, t, :], mood_sb)
+        woven2, codes2, scales2 = weave(pairs2, "2")
 
         def score(b, codes, scales):
             e = bank(b)
@@ -176,15 +204,24 @@ def tile_list_dorm_bed_scores_kernel(tc, tab_words, tab_scales, tab2_words, tab2
                                 rhs=codes[:].bitcast(FP8X4), rhs_scale=scales[:], start=True, stop=True)
             return e
 
-        for b in range(M_TILES):
-            e2 = score(b, codes2, scales2)
-            nc.vector.scalar_tensor_tensor(out=quiet_sb[:, b, :], in0=quiet_sb[:, b, :], scalar=care_sb[:, b: b + 1],
-                                           in1=e2[:], op0=ALU.mult, op1=ALU.add)
-            if b == 5:
-                nc.vector.quantize_mx(out=codes1[:].bitcast(FP8X4), scales=scales1[:], in_=woven1[:])
+        own = M_TILES - POOL_TILES
         for b in range(M_TILES):
             e1 = score(b, codes1, scales1)
-            res = ring.tile([P, PAIRS], F32, name="res", bufs=M_TILES)
-            nc.vector.scalar_tensor_tensor(out=res[:], in0=e1[:], scalar=care_sb[:, b: b + 1],
-                                           in1=quiet_sb[:, b, :], op0=ALU.mult, op1=ALU.add)
+            if b < own:
+                nc.vector.tensor_tensor(out=quiet_sb[:, b, :], in0=e1[:], in1=quiet_sb[:, b, :], op=ALU.add)
+            else:
+                staged = keep.tile([P, PAIRS], F32, name="woven1" if b == own else "staged%d" % b,
+                                   align_bytes=64)
+                nc.scalar.copy(out=staged[:], in_=e1[:])
+                for u in range(2):
+                    cols = slice(u * PAIRS // 2, (u + 1) * PAIRS // 2)
+                    nc.gpsimd.tensor_tensor(out=quiet_sb[:, b, cols], in0=staged[:, cols], in1=quiet_sb[:, b, cols],
+                                            op=ALU.add)
+            if b == min(own - 1, 5):
+                nc.vector.quantize_mx(out=codes2[:].bitcast(FP8X4), scales=scales2[:], in_=woven2[:])
+        for b in range(M_TILES):
+            e2 = score(b, codes2, scales2)
+            res = ring.tile([P, PAIRS], F32, name="res", bufs=6)
+            nc.vector.scalar_tensor_tensor(out=res[:], in0=quiet_sb[:, b, :], scalar=care_sb[:, b: b + 1],
+                                           in1=e2[:], op0=ALU.mult, op1=ALU.add)
             nc.sync.dma_start(out=out[b * P: (b + 1) * P, :], in_=res[:])

@@ -68,27 +68,27 @@ def tile_list_dorm_bed_scores_kernel(tc, tab_words, tab_scales, tab2_words, tab2
             nc.sync.dma_start(out=dst[:],
                               in_=w1[a * P * PACK: (a + 1) * P * PACK, cols].rearrange("(p j) c -> p j c", j=PACK))
 
-        nc.sync.dma_start(idx[:], offs)
-        load_words(0, slice(0, T // 2))
         for q in range(QUADS):
-            nc.sync.dma_start(out=v_scales[32 * q: 32 * q + 4 * PASSES, :].bitcast(I32),
-                              in_=tab_scales[:, 4 * q: 4 * q + 4, :].bitcast(I32))
-        load_words(0, slice(T // 2, T))
+            nc.gpsimd.dma_start(out=v_scales[32 * q: 32 * q + 4 * PASSES, :].bitcast(I32),
+                                in_=tab_scales[:, 4 * q: 4 * q + 4, :].bitcast(I32))
         nc.sync.dma_start(idx2[:], offs2)
+        load_words(0, slice(0, T // 2))
+        v2_rows = tab2_scales[0].rearrange("(q r) n -> r q n", r=4)
+        for r in range(4):
+            nc.sync.dma_start(out=v2_scales[V2_ROW + r: P: 32, :].bitcast(I32), in_=v2_rows[r].bitcast(I32))
+        load_words(0, slice(T // 2, T))
+        nc.sync.dma_start(idx[:], offs)
         load_w1(w_first, 0, slice(0, H))
-        for q in range(QUADS):
-            nc.sync.dma_start(out=v2_scales[32 * q + V2_ROW: 32 * q + V2_ROW + 4, :].bitcast(I32),
-                              in_=tab2_scales[0, 4 * q: 4 * q + 4, :].bitcast(I32))
-        load_words(1, slice(0, T))
-        for u in range(2):
-            load_w1(w_last[u], 1, slice(u * H // 2, (u + 1) * H // 2))
-        nc.sync.dma_start(out=v2_words[:].bitcast(I32),
-                          in_=tab2_words[0].rearrange("p n i -> p (n i)").bitcast(I32))
         nc.sync.dma_start(p1[:], pos1)
         nc.sync.dma_start(p2[:], pos2)
         nc.sync.dma_start(out=gain_sb[:], in_=gain.rearrange("(p t) -> p t", t=PACK))
         nc.sync.dma_start(out=mood_sb[:], in_=mood.rearrange("(p t) -> p t", t=PACK))
         nc.sync.dma_start(out=care_rows[0:M_TILES, :], in_=care.rearrange("(b p) -> b p", p=P))
+        load_words(1, slice(0, T))
+        for u in range(2):
+            load_w1(w_last[u], 1, slice(u * H // 2, (u + 1) * H // 2))
+        nc.sync.dma_start(out=v2_words[:].bitcast(I32),
+                          in_=tab2_words[0].rearrange("p n i -> p (n i)").bitcast(I32))
         nc.sync.dma_start(out=plans_sb[:], in_=plans.rearrange("(p t) j -> p t j", t=PACK))
         nc.sync.dma_start(out=quiet_sb[:], in_=quiet.rearrange("(b p) j -> p b j", p=P))
 
@@ -103,12 +103,12 @@ def tile_list_dorm_bed_scores_kernel(tc, tab_words, tab_scales, tab2_words, tab2
         w_codes = [keep.tile([P, H], U32, name="w_codes%d" % a, align_bytes=64) for a in range(PASSES)]
         w_scales = [keep.tile([P, H], U8, name="w_scales%d" % a, align_bytes=64) for a in range(PASSES)]
 
-        nc.vector.tensor_copy(vg_scales[:], v_scales[:].indirect(idx[:]))
+        nc.vector.tensor_copy(v2g_scales[:], v2_scales[:].indirect(idx2[:]))
         z = [[bank(2 * t + s) for s in range(2)] for t in range(PACK)]
         for a in range(PASSES):
             nc.vector.tensor_copy(vg_words[a][:], v_words[a][:].indirect(idx[:]))
             if a == 0:
-                nc.vector.tensor_copy(v2g_scales[:], v2_scales[:].indirect(idx2[:]))
+                nc.vector.tensor_copy(vg_scales[:], v_scales[:].indirect(idx[:]))
             dst = w_bf[a][:].rearrange("p (t m j) -> p m j t", t=PACK, j=PACK)
             if a == 0:
                 nc.scalar.copy(out=dst, in_=w_first[:].rearrange("p j (m t) -> p m j t", t=PACK))

@@ -24,8 +24,8 @@ PASSES = K // (P * PACK)
 M_TILES = S2 // P
 QUADS = 4
 V2_ROW = 8
-M_SPLIT = 40
-POOL_TILES = 0
+M_SPLIT = 80
+POOL_TILES = 3
 
 
 def tile_list_dorm_bed_scores_kernel(tc, tab_words, tab_scales, tab2_words, tab2_scales, offs, offs2,
@@ -46,8 +46,7 @@ def tile_list_dorm_bed_scores_kernel(tc, tab_words, tab_scales, tab2_words, tab2
         v_scales = keep.tile([P, T], U8, name="v_scales")
         v2_words = keep.tile([P, T3], U32, name="v2_words")
         v2_scales = keep.tile([P, T3], U8, name="v2_scales")
-        w_first = keep.tile([P, PACK, H], F32, name="w_first")
-        w_last = [keep.tile([P, PACK, H // 2], F32, name="w_last%d" % u) for u in range(2)]
+        w_raw = [keep.tile([P, PACK, H], F32, name="w_raw%d" % a) for a in range(PASSES)]
         gain_sb = keep.tile([P, PACK], F32, name="gain_sb")
         mood_sb = keep.tile([P, PACK], F32, name="mood_sb")
         plans_sb = keep.tile([P, PACK, PAIRS], F32, name="plans_sb")
@@ -64,31 +63,33 @@ def tile_list_dorm_bed_scores_kernel(tc, tab_words, tab_scales, tab2_words, tab2
             nc.sync.dma_start(out=v_words[a][:, cols].bitcast(I32),
                               in_=tab_words[a].rearrange("p n i -> p (n i)").bitcast(I32)[:, cols])
 
-        def load_w1(dst, a, cols):
-            nc.sync.dma_start(out=dst[:],
-                              in_=w1[a * P * PACK: (a + 1) * P * PACK, cols].rearrange("(p j) c -> p j c", j=PACK))
+        def load_w1(a):
+            nc.sync.dma_start(out=w_raw[a][:],
+                              in_=w1[a * P * PACK: (a + 1) * P * PACK, :].rearrange("(p j) c -> p j c", j=PACK))
 
-        for q in range(QUADS):
-            nc.gpsimd.dma_start(out=v_scales[32 * q: 32 * q + 4 * PASSES, :].bitcast(I32),
-                                in_=tab_scales[:, 4 * q: 4 * q + 4, :].bitcast(I32))
-        nc.sync.dma_start(idx2[:], offs2)
-        load_words(0, slice(0, T // 2))
-        v2_rows = tab2_scales[0].rearrange("(q r) n -> r q n", r=4)
-        for r in range(4):
-            nc.sync.dma_start(out=v2_scales[V2_ROW + r: P: 32, :].bitcast(I32), in_=v2_rows[r].bitcast(I32))
-        load_words(0, slice(T // 2, T))
+        def load_scale_row(plane, first, rows, r):
+            nc.sync.dma_start(out=plane[first + r: P: 32, :].bitcast(I32),
+                              in_=rows.rearrange("(q r) n -> r q n", r=4)[r].bitcast(I32))
+
         nc.sync.dma_start(idx[:], offs)
-        load_w1(w_first, 0, slice(0, H))
+        load_words(0, slice(0, T // 2))
+        for q in range(QUADS):
+            nc.sync.dma_start(out=v_scales[32 * q: 32 * q + 4 * PASSES, :].bitcast(I32),
+                              in_=tab_scales[:, 4 * q: 4 * q + 4, :].bitcast(I32))
+        load_words(0, slice(T // 2, T))
+        nc.sync.dma_start(idx2[:], offs2)
+        load_w1(0)
+        for r in range(4):
+            load_scale_row(v2_scales, V2_ROW, tab2_scales[0], r)
+        load_words(1, slice(0, T))
+        load_w1(1)
+        nc.sync.dma_start(out=v2_words[:].bitcast(I32),
+                          in_=tab2_words[0].rearrange("p n i -> p (n i)").bitcast(I32))
         nc.sync.dma_start(p1[:], pos1)
         nc.sync.dma_start(p2[:], pos2)
         nc.sync.dma_start(out=gain_sb[:], in_=gain.rearrange("(p t) -> p t", t=PACK))
         nc.sync.dma_start(out=mood_sb[:], in_=mood.rearrange("(p t) -> p t", t=PACK))
         nc.sync.dma_start(out=care_rows[0:M_TILES, :], in_=care.rearrange("(b p) -> b p", p=P))
-        load_words(1, slice(0, T))
-        for u in range(2):
-            load_w1(w_last[u], 1, slice(u * H // 2, (u + 1) * H // 2))
-        nc.sync.dma_start(out=v2_words[:].bitcast(I32),
-                          in_=tab2_words[0].rearrange("p n i -> p (n i)").bitcast(I32))
         nc.sync.dma_start(out=plans_sb[:], in_=plans.rearrange("(p t) j -> p t j", t=PACK))
         nc.sync.dma_start(out=quiet_sb[:], in_=quiet.rearrange("(b p) j -> p b j", p=P))
 
@@ -103,22 +104,20 @@ def tile_list_dorm_bed_scores_kernel(tc, tab_words, tab_scales, tab2_words, tab2
         w_codes = [keep.tile([P, H], U32, name="w_codes%d" % a, align_bytes=64) for a in range(PASSES)]
         w_scales = [keep.tile([P, H], U8, name="w_scales%d" % a, align_bytes=64) for a in range(PASSES)]
 
-        nc.vector.tensor_copy(v2g_scales[:], v2_scales[:].indirect(idx2[:]))
         z = [[bank(2 * t + s) for s in range(2)] for t in range(PACK)]
+        nc.vector.tensor_copy(vg_scales[:], v_scales[:].indirect(idx[:]))
         for a in range(PASSES):
             nc.vector.tensor_copy(vg_words[a][:], v_words[a][:].indirect(idx[:]))
             if a == 0:
-                nc.vector.tensor_copy(vg_scales[:], v_scales[:].indirect(idx[:]))
+                nc.vector.tensor_copy(v2g_scales[:], v2_scales[:].indirect(idx2[:]))
             dst = w_bf[a][:].rearrange("p (t m j) -> p m j t", t=PACK, j=PACK)
+            src = w_raw[a][:].rearrange("p j (m t) -> p m j t", t=PACK)
             if a == 0:
-                nc.scalar.copy(out=dst, in_=w_first[:].rearrange("p j (m t) -> p m j t", t=PACK))
+                nc.scalar.copy(out=dst, in_=src)
                 nc.vector.quantize_mx(out=w_codes[a][:].bitcast(FP8X4), scales=w_scales[a][:], in_=w_bf[a][:])
             else:
-                src = [w[:].rearrange("p j (m t) -> p m j t", t=PACK) for w in w_last]
-                half = P // 2
-                nc.scalar.copy(out=dst[:, :half], in_=src[0])
-                nc.vector.tensor_copy(out=dst[:, half: half + M_SPLIT], in_=src[1][:, :M_SPLIT])
-                nc.scalar.copy(out=dst[:, half + M_SPLIT:], in_=src[1][:, M_SPLIT:])
+                nc.vector.tensor_copy(out=dst[:, :M_SPLIT], in_=src[:, :M_SPLIT])
+                nc.scalar.copy(out=dst[:, M_SPLIT:], in_=src[:, M_SPLIT:])
             for t in range(PACK):
                 cols = slice(t * P, (t + 1) * P)
                 if a == 1:
@@ -138,7 +137,6 @@ def tile_list_dorm_bed_scores_kernel(tc, tab_words, tab_scales, tab2_words, tab2
         for s in range(2):
             nc.vector.tensor_scalar(out=whole0[s][:], in0=z[0][s][:], scalar1=per_turn, scalar2=0.25,
                                     op0=ALU.mult, op1=ALU.add)
-        for s in range(2):
             frac0 = ring.tile([P, BANK], F32, name="turns")
             nc.vector.scalar_tensor_tensor(out=frac0[:], in0=z[0][s][:], scalar=per_turn, in1=whole0[s][:],
                                            op0=ALU.mult, op1=ALU.subtract)
@@ -185,15 +183,16 @@ def tile_list_dorm_bed_scores_kernel(tc, tab_words, tab_scales, tab2_words, tab2
 
         pairs2 = keep.tile([P, 2, PAIRS, 2], BF16, name="pairs2")
         for t in range(PACK):
+            g2 = keep.tile([P, PAIRS], F32, name="frac3" if t == 2 else "g2_%d" % t)
+            nc.vector.tensor_copy(g2[:], cosz[t][:].indirect(p2[:]))
+            summed = plans_sb[:, t, :]
             if t == 3:
                 nc.vector.quantize_mx(out=codes1[:].bitcast(FP8X4), scales=scales1[:], in_=woven1[:])
-                g2 = keep.tile([P, PAIRS], F32, name="woven1", align_bytes=64)
-            else:
-                g2 = keep.tile([P, PAIRS], F32, name="frac3" if t == 2 else "g2_%d" % t)
-            nc.vector.tensor_copy(g2[:], cosz[t][:].indirect(p2[:]))
-            nc.vector.scalar_tensor_tensor(out=plans_sb[:, t, :], in0=g2[:], scalar=gain_sb[:, t: t + 1],
+                last_sum = keep.tile([P, PAIRS], F32, name="woven1", align_bytes=64)
+                summed = last_sum[:]
+            nc.vector.scalar_tensor_tensor(out=summed, in0=g2[:], scalar=gain_sb[:, t: t + 1],
                                            in1=plans_sb[:, t, :], op0=ALU.mult, op1=ALU.add)
-            round_into(pairs2, t, plans_sb[:, t, :], mood_sb)
+            round_into(pairs2, t, summed, mood_sb)
         woven2, codes2, scales2 = weave(pairs2, "2")
 
         def score(b, codes, scales):
@@ -205,19 +204,16 @@ def tile_list_dorm_bed_scores_kernel(tc, tab_words, tab_scales, tab2_words, tab2
             return e
 
         own = M_TILES - POOL_TILES
+        staged_all = keep.tile([P, POOL_TILES, PAIRS], F32, name="pairs2")
         for b in range(M_TILES):
             e1 = score(b, codes1, scales1)
             if b < own:
                 nc.vector.tensor_tensor(out=quiet_sb[:, b, :], in0=e1[:], in1=quiet_sb[:, b, :], op=ALU.add)
             else:
-                staged = keep.tile([P, PAIRS], F32, name="woven1" if b == own else "staged%d" % b,
-                                   align_bytes=64)
-                nc.scalar.copy(out=staged[:], in_=e1[:])
-                for u in range(2):
-                    cols = slice(u * PAIRS // 2, (u + 1) * PAIRS // 2)
-                    nc.gpsimd.tensor_tensor(out=quiet_sb[:, b, cols], in0=staged[:, cols], in1=quiet_sb[:, b, cols],
-                                            op=ALU.add)
-            if b == min(own - 1, 5):
+                staged = staged_all[:, b - own, :]
+                nc.scalar.copy(out=staged, in_=e1[:])
+                nc.gpsimd.tensor_tensor(out=quiet_sb[:, b, :], in0=staged, in1=quiet_sb[:, b, :], op=ALU.add)
+            if b == own - 2:
                 nc.vector.quantize_mx(out=codes2[:].bitcast(FP8X4), scales=scales2[:], in_=woven2[:])
         for b in range(M_TILES):
             e2 = score(b, codes2, scales2)

import math
from contextlib import ExitStack

import concourse.mybir as mybir
from concourse.masks import make_identity

K, T, S, H, T3, S2, PAIRS = 1024, 4096, 1024, 512, 2048, 1024, 512
FLOPS = 2 * K * H * S + 2 * 2 * H * S2 * PAIRS

F32 = mybir.dt.float32
BF16 = mybir.dt.bfloat16
I32 = mybir.dt.int32
U32 = mybir.dt.uint32
U16 = mybir.dt.uint16
U8 = mybir.dt.uint8
FP8X4 = mybir.dt.float8_e4m3fn_x4
ALU = mybir.AluOpType
ACT = mybir.ActivationFunctionType

P = 128
PACK = 4
BANK = 512
PASSES = K // (P * PACK)
M_TILES = S2 // P
QUADS = 4
V2_ROW = 8
M_SPLIT = 80
POOL_TILES = 3


def tile_list_dorm_bed_scores_kernel(tc, tab_words, tab_scales, tab2_words, tab2_scales, offs, offs2,
                                               pos1, pos2, w1, gain, plans, mood, quiet, care, out):
    nc = tc.nc
    with ExitStack() as ctx:
        lists = ctx.enter_context(tc.tile_pool(name="lists", bufs=1))
        keep = ctx.enter_context(tc.tile_pool(name="keep", bufs=1))
        ring = ctx.enter_context(tc.tile_pool(name="ring", bufs=2))
        psum = ctx.enter_context(tc.psum_pool(name="psum", bufs=1))

        idx = lists.tile([P, S // 16], U16, name="idx")
        idx2 = lists.tile([P, S2 // 16], U16, name="idx2")
        p1 = lists.tile([P, PAIRS // 16], U16, name="p1")
        p2 = lists.tile([P, PAIRS // 16], U16, name="p2")

        v_words = [keep.tile([P, T], U32, name="v_words%d" % a) for a in range(PASSES)]
        v_scales = keep.tile([P, T], U8, name="v_scales")
        v2_words = keep.tile([P, T3], U32, name="v2_words")
        v2_scales = keep.tile([P, T3], U8, name="v2_scales")
        w_raw = [keep.tile([P, PACK, H], F32, name="w_raw%d" % a) for a in range(PASSES)]
        gain_sb = keep.tile([P, PACK], F32, name="gain_sb")
        mood_sb = keep.tile([P, PACK], F32, name="mood_sb")
        plans_sb = keep.tile([P, PACK, PAIRS], F32, name="plans_sb")
        quiet_sb = keep.tile([P, M_TILES, PAIRS], F32, name="quiet_sb")
        care_rows = keep.tile([P, P], F32, name="care_rows")
        ident = keep.tile([P, P], F32, name="ident")

        nc.vector.memset(v_scales[:].bitcast(I32), 0)
        nc.vector.memset(v2_scales[:].bitcast(I32), 0)
        nc.vector.memset(care_rows[:], 0.0)
        make_identity(nc, ident[:])

        def load_words(a, cols):
            nc.sync.dma_start(out=v_words[a][:, cols].bitcast(I32),
                              in_=tab_words[a].rearrange("p n i -> p (n i)").bitcast(I32)[:, cols])

        def load_w1(a):
            nc.sync.dma_start(out=w_raw[a][:],
                              in_=w1[a * P * PACK: (a + 1) * P * PACK, :].rearrange("(p j) c -> p j c", j=PACK))

        def load_scale_row(plane, first, rows, r):
            nc.sync.dma_start(out=plane[first + r: P: 32, :].bitcast(I32),
                              in_=rows.rearrange("(q r) n -> r q n", r=4)[r].bitcast(I32))

        nc.sync.dma_start(idx[:], offs)
        load_words(0, slice(0, T // 2))
        for q in range(QUADS):
            nc.sync.dma_start(out=v_scales[32 * q: 32 * q + 4 * PASSES, :].bitcast(I32),
                              in_=tab_scales[:, 4 * q: 4 * q + 4, :].bitcast(I32))
        load_words(0, slice(T // 2, T))
        nc.sync.dma_start(idx2[:], offs2)
        load_w1(0)
        for r in range(4):
            load_scale_row(v2_scales, V2_ROW, tab2_scales[0], r)
        load_words(1, slice(0, T))
        load_w1(1)
        nc.sync.dma_start(out=v2_words[:].bitcast(I32),
                          in_=tab2_words[0].rearrange("p n i -> p (n i)").bitcast(I32))
        nc.sync.dma_start(p1[:], pos1)
        nc.sync.dma_start(p2[:], pos2)
        nc.sync.dma_start(out=gain_sb[:], in_=gain.rearrange("(p t) -> p t", t=PACK))
        nc.sync.dma_start(out=mood_sb[:], in_=mood.rearrange("(p t) -> p t", t=PACK))
        nc.sync.dma_start(out=care_rows[0:M_TILES, :], in_=care.rearrange("(b p) -> b p", p=P))
        nc.sync.dma_start(out=plans_sb[:], in_=plans.rearrange("(p t) j -> p t j", t=PACK))
        nc.sync.dma_start(out=quiet_sb[:], in_=quiet.rearrange("(b p) j -> p b j", p=P))

        def bank(b):
            return psum.tile([P, BANK], F32, name="bank%d" % b)

        vg_scales = keep.tile([P, S], U8, name="vg_scales", align_bytes=64)
        v2g_scales = keep.tile([P, S2], U8, name="v2g_scales", align_bytes=64)
        vg_words = [keep.tile([P, S], U32, name="vg_words%d" % a, align_bytes=64) for a in range(PASSES)]
        v2g_words = keep.tile([P, S2], U32, name="v2g_words", align_bytes=64)
        w_bf = [keep.tile([P, PACK * H], BF16, name="w_bf%d" % a, align_bytes=64) for a in range(PASSES)]
        w_codes = [keep.tile([P, H], U32, name="w_codes%d" % a, align_bytes=64) for a in range(PASSES)]
        w_scales = [keep.tile([P, H], U8, name="w_scales%d" % a, align_bytes=64) for a in range(PASSES)]

        z = [[bank(2 * t + s) for s in range(2)] for t in range(PACK)]
        nc.vector.tensor_copy(vg_scales[:], v_scales[:].indirect(idx[:]))
        for a in range(PASSES):
            nc.vector.tensor_copy(vg_words[a][:], v_words[a][:].indirect(idx[:]))
            if a == 0:
                nc.vector.tensor_copy(v2g_scales[:], v2_scales[:].indirect(idx2[:]))
            dst = w_bf[a][:].rearrange("p (t m j) -> p m j t", t=PACK, j=PACK)
            src = w_raw[a][:].rearrange("p j (m t) -> p m j t", t=PACK)
            if a == 0:
                nc.scalar.copy(out=dst, in_=src)
                nc.vector.quantize_mx(out=w_codes[a][:].bitcast(FP8X4), scales=w_scales[a][:], in_=w_bf[a][:])
            else:
                nc.vector.tensor_copy(out=dst[:, :M_SPLIT], in_=src[:, :M_SPLIT])
                nc.scalar.copy(out=dst[:, M_SPLIT:], in_=src[:, M_SPLIT:])
            for t in range(PACK):
                cols = slice(t * P, (t + 1) * P)
                if a == 1:
                    nc.vector.quantize_mx(out=w_codes[a][:, cols].bitcast(FP8X4), scales=w_scales[a][:, cols],
                                          in_=w_bf[a][:, t * BANK: (t + 1) * BANK])
                for s in range(2):
                    n = slice(s * BANK, (s + 1) * BANK)
                    nc.tensor.matmul_mx(out=z[t][s][:], lhsT=w_codes[a][:, cols].bitcast(FP8X4),
                                        lhsT_scale=w_scales[a][:, cols],
                                        rhs=vg_words[a][:, n].bitcast(FP8X4), rhs_scale=vg_scales[4 * a:, n],
                                        start=(a == 0), stop=(a == PASSES - 1))


        per_turn = 1.0 / (2.0 * math.pi)
        cosz = [keep.tile([P, S], F32, name="cosz%d" % t) for t in range(PACK)]
        whole0 = [keep.tile([P, BANK], I32, name="whole0_%d" % s) for s in range(2)]
        for s in range(2):
            nc.vector.tensor_scalar(out=whole0[s][:], in0=z[0][s][:], scalar1=per_turn, scalar2=0.25,
                                    op0=ALU.mult, op1=ALU.add)
            frac0 = ring.tile([P, BANK], F32, name="turns")
            nc.vector.scalar_tensor_tensor(out=frac0[:], in0=z[0][s][:], scalar=per_turn, in1=whole0[s][:],
                                           op0=ALU.mult, op1=ALU.subtract)
            nc.scalar.activation(out=cosz[0][:, s * BANK: (s + 1) * BANK], in_=frac0[:], func=ACT.Sin,
                                 scale=2.0 * math.pi, bias=0.5 * math.pi)
        nc.vector.tensor_copy(v2g_words[:], v2_words[:].indirect(idx2[:]))
        fracs = {}
        for t in range(1, PACK):
            turns = ring.tile([P, S], F32, name="turns")
            for s in range(2):
                nc.scalar.activation(out=turns[:, s * BANK: (s + 1) * BANK], in_=z[t][s][:], func=ACT.Abs,
                                     scale=per_turn)
            whole = keep.tile([P, S], U32, name="whole%d" % t)
            nc.scalar.activation(out=whole[:], in_=turns[:], func=ACT.Copy, bias=0.25)
            fracs[t] = keep.tile([P, S], F32, name="frac%d" % t)
            nc.vector.scalar_tensor_tensor(out=fracs[t][:], in0=turns[:], scalar=0.25, in1=whole[:].bitcast(I32),
                                           op0=ALU.add, op1=ALU.subtract)
        for t in range(1, PACK):
            nc.scalar.activation(out=cosz[t][:], in_=fracs[t][:], func=ACT.Sin, scale=2.0 * math.pi)

        care_ps = bank(0)
        nc.tensor.transpose(care_ps[:, 0:P], care_rows[:], ident[:])
        care_sb = keep.tile([P, M_TILES], F32, name="care_sb")
        nc.scalar.copy(out=care_sb[:], in_=care_ps[:, 0:M_TILES])

        def round_into(pairs, t, values, factor):
            nc.scalar.activation(out=pairs[:, t // 2, :, t % 2], in_=values, func=ACT.Copy,
                                 scale=factor[:, t: t + 1])

        def weave(pairs, tag):
            woven = keep.tile([P, PACK * PAIRS], BF16, name="woven" + tag, align_bytes=64)
            nc.scalar.copy(out=woven[:].bitcast(U32).rearrange("p (j h) -> p j h", h=2),
                           in_=pairs[:].rearrange("p h j e -> p h (j e)").bitcast(U32).rearrange("p h j -> p j h"))
            codes = keep.tile([P, PAIRS], U32, name="codes" + tag, align_bytes=64)
            scales = keep.tile([P, PAIRS], U8, name="scales" + tag, align_bytes=64)
            return woven, codes, scales

        pairs1 = keep.tile([P, 2, PAIRS, 2], BF16, name="pairs1")
        for t in range(PACK):
            g1 = keep.tile([P, PAIRS], F32, name="whole1" if t == 0 else "g1_%d" % t)
            nc.vector.tensor_copy(g1[:], cosz[t][:].indirect(p1[:]))
            round_into(pairs1, t, g1[:], gain_sb)
        woven1, codes1, scales1 = weave(pairs1, "1")

        pairs2 = keep.tile([P, 2, PAIRS, 2], BF16, name="pairs2")
        for t in range(PACK):
            g2 = keep.tile([P, PAIRS], F32, name="frac3" if t == 2 else "g2_%d" % t)
            nc.vector.tensor_copy(g2[:], cosz[t][:].indirect(p2[:]))
            summed = plans_sb[:, t, :]
            if t == 3:
                nc.vector.quantize_mx(out=codes1[:].bitcast(FP8X4), scales=scales1[:], in_=woven1[:])
                last_sum = keep.tile([P, PAIRS], F32, name="woven1", align_bytes=64)
                summed = last_sum[:]
            nc.vector.scalar_tensor_tensor(out=summed, in0=g2[:], scalar=gain_sb[:, t: t + 1],
                                           in1=plans_sb[:, t, :], op0=ALU.mult, op1=ALU.add)
            round_into(pairs2, t, summed, mood_sb)
        woven2, codes2, scales2 = weave(pairs2, "2")

        def score(b, codes, scales):
            e = bank(b)
            cols = slice(b * P, (b + 1) * P)
            nc.tensor.matmul_mx(out=e[:], lhsT=v2g_words[:, cols].bitcast(FP8X4),
                                lhsT_scale=v2g_scales[V2_ROW:, cols],
                                rhs=codes[:].bitcast(FP8X4), rhs_scale=scales[:], start=True, stop=True)
            return e

        own = M_TILES - POOL_TILES
        staged_all = keep.tile([P, POOL_TILES, PAIRS], F32, name="pairs2")
        for b in range(M_TILES):
            e1 = score(b, codes1, scales1)
            if b < own:
                nc.vector.tensor_tensor(out=quiet_sb[:, b, :], in0=e1[:], in1=quiet_sb[:, b, :], op=ALU.add)
            else:
                staged = staged_all[:, b - own, :]
                nc.scalar.copy(out=staged, in_=e1[:])
                nc.gpsimd.tensor_tensor(out=quiet_sb[:, b, :], in0=staged, in1=quiet_sb[:, b, :], op=ALU.add)
            if b == own - 2:
                nc.vector.quantize_mx(out=codes2[:].bitcast(FP8X4), scales=scales2[:], in_=woven2[:])
        for b in range(M_TILES):
            e2 = score(b, codes2, scales2)
            res = ring.tile([P, PAIRS], F32, name="res", bufs=6)
            nc.vector.scalar_tensor_tensor(out=res[:], in0=quiet_sb[:, b, :], scalar=care_sb[:, b: b + 1],
                                           in1=e2[:], op0=ALU.mult, op1=ALU.add)
            nc.sync.dma_start(out=out[b * P: (b + 1) * P, :], in_=res[:])
